import numpy as np
import ml_dtypes


def mxq(x, axis, fmt="e4m3"):
    dtype, down = {"e4m3": (ml_dtypes.float8_e4m3fn, 7), "e5m2": (ml_dtypes.float8_e5m2, 14)}[fmt]
    v = np.moveaxis(np.asarray(x, np.float32).astype(ml_dtypes.bfloat16).astype(np.float64), axis, -1)
    blocks = v.reshape(v.shape[:-1] + (-1, 32))
    amax = np.abs(blocks).max(-1, keepdims=True)
    byte = np.maximum(np.where(amax > 0, np.frexp(amax)[1] - 1 + 127, 0) - down, 1)
    scale = np.exp2(byte - 127.0)
    codes = (blocks / scale).astype(np.float32).astype(dtype).astype(np.float64)
    return np.moveaxis((codes * scale).reshape(v.shape), -1, axis)


WIDE = False


def mx_kscale(k):
    if not WIDE:
        return np.ones(k)
    levels = np.array([10, -10, 5, -5, 0])
    if k % 512:
        return np.exp2(np.random.permutation(np.resize(levels, k // 32))).repeat(32)
    a = np.empty((k // 512, 16))
    for p in range(k // 512):
        a[p, :8] = np.random.permutation(np.resize(levels, 8))
        for g in range(8):
            far = levels[np.abs(levels - a[p, g]) >= 10]
            a[p, g + 8] = far[np.random.randint(len(far))]
    return np.exp2(a.ravel()).repeat(32)


def f64(x):
    return np.asarray(x).astype(np.float64)


def striped(idx):
    return np.tile(idx.reshape(-1, 16).T, (8, 1)).astype(np.uint16)


def unstriped(offs):
    return offs[:16].T.reshape(-1).astype(np.int64)


def striped8(idx):
    return np.concatenate([x.reshape(-1, 16).T for x in idx]).astype(np.uint16)


def runs(offs, k):
    lists = np.stack([offs[16 * r : 16 * r + 16].T.reshape(-1) for r in range(8)]).astype(np.int64)
    return lists[np.arange(k) % 512 // 64]


def pack_weight(w):
    k, n = w.shape
    w = f64(np.asarray(w, np.float32).astype(ml_dtypes.bfloat16)).reshape(k // 32, 32, n)
    amax = np.abs(w).max(1)
    byte = np.clip(np.where(amax > 0, np.frexp(amax)[1] - 1 + 127 - 7, 1), 1, 254)
    scaled = (w * np.exp2(127.0 - byte)[:, None, :]).reshape(k, n).astype(np.float32)
    words = np.ascontiguousarray(scaled.reshape(k // 512, 128, 4, n).transpose(0, 1, 3, 2)).astype(ml_dtypes.float8_e4m3fn).view(np.uint8)
    return words, np.ascontiguousarray(byte.astype(np.uint8).reshape(k // 512, 16, n))


def unpack_weight(words, scales):
    g, p, n, _ = words.shape
    vals = np.ascontiguousarray(words).view(ml_dtypes.float8_e4m3fn).astype(np.float64) * np.repeat(np.exp2(scales.astype(np.float64) - 127.0), 8, axis=1)[..., None]
    return vals.transpose(0, 1, 3, 2).reshape(g * 512, n)


K, T, S, N, G, H = 512, 2048, 512, 512, 2048, 512


def setup_inputs():
    n = np.random.standard_normal
    s = mx_kscale(K)[:, None]
    u = mx_kscale(S)
    packed_xT = pack_weight(n((K, T)) * s)
    packed_dT = pack_weight(n((K, G)) / s)
    return {
        "x_words": packed_xT[0],
        "x_scales": packed_xT[1],
        "d_words": packed_dT[0],
        "d_scales": packed_dT[1],
        "gn": (np.random.uniform(0.5, 1.5, (H, 1)) * u[:, None]).astype(np.float32),
        "w1": (n((H, N)) / np.sqrt(H) / u[:, None]).astype(np.float32),
        "offs": striped(np.random.permutation(T)[:S]),
        "kidx": striped8(np.random.randint(0, G, (8, H))),
        "n1": striped8(np.stack([np.random.permutation(S) for _ in range(8)])),
        "n2": striped8(np.stack([np.random.permutation(S) for _ in range(8)])),
    }


def reference(x_words, x_scales, d_words, d_scales, gn, w1, offs, kidx, n1, n2):
    d_kidx = unpack_weight(d_words, d_scales)[np.arange(K)[:, None], runs(kidx, K)]
    xq = unpack_weight(x_words, x_scales)[:, unstriped(offs)]
    s = 0.0625 * (d_kidx.T @ xq)
    z = f64(gn) * (s - (s[np.arange(H)[:, None], runs(n1, H)]))
    h = mxq(f64(w1), 0, "e4m3").T @ mxq(z, 0, "e4m3")
    return np.maximum(h, h[np.arange(N)[:, None], runs(n2, N)])

@@ -1,0 +1,172 @@
+from contextlib import ExitStack
+
+import concourse.mybir as mybir
+
+F32 = mybir.dt.float32
+BF16 = mybir.dt.bfloat16
+I32 = mybir.dt.int32
+U32 = mybir.dt.uint32
+U16 = mybir.dt.uint16
+U8 = mybir.dt.uint8
+FP8X4 = mybir.dt.float8_e4m3fn_x4
+COPY = mybir.ActivationFunctionType.Copy
+ALU = mybir.AluOpType
+
+P = 128
+PACK = 4
+TABLE = 2048
+S = 512
+HALF = S // 2
+LINE = 4
+
+FLOPS = 2 * 2 * 512 * 512 * 512
+
+
+def tile_picked_keydifbig_none_p_kernel(
+    tc, x_words, x_scales, d_words, d_scales, gn, w1, offs, kidx, n1, n2, out
+):
+    nc = tc.nc
+    with ExitStack() as ctx:
+        lists = ctx.enter_context(tc.tile_pool(name="lists", bufs=1))
+        keep = ctx.enter_context(tc.tile_pool(name="keep", bufs=1))
+        psum = ctx.enter_context(tc.psum_pool(name="psum", bufs=1))
+
+        d_scale_tab = keep.tile([P, TABLE], U8, name="d_scale_tab", tag="early_small")
+        x_scale_tab = keep.tile([P, TABLE], U8, name="x_scale_tab")
+        nc.vector.memset(d_scale_tab[:].bitcast(I32), 0)
+        nc.vector.memset(x_scale_tab[:].bitcast(I32), 0)
+
+        kidx_sb = lists.tile([P, S // 16], U16, name="kidx_sb")
+        offs_sb = lists.tile([P, S // 16], U16, name="offs_sb")
+        n1_sb = lists.tile([P, S // 16], U16, name="n1_sb")
+        n2_sb = lists.tile([P, S // 16], U16, name="n2_sb")
+        nc.sync.dma_start(kidx_sb[:], kidx)
+        nc.sync.dma_start(offs_sb[:], offs)
+
+        nc.scalar.dma_start(d_scale_tab[0:P:8, :].bitcast(I32), d_scales[0].bitcast(I32))
+        nc.scalar.dma_start(x_scale_tab[0:P:8, :].bitcast(I32), x_scales[0].bitcast(I32))
+
+        d_tab = keep.tile([P, TABLE], U32, name="d_tab", tag="early_big")
+        x_tab = keep.tile([P, TABLE], U32, name="x_tab")
+        nc.sync.dma_start(d_tab[:].bitcast(I32), d_words[0].rearrange("p n t -> p (n t)").bitcast(I32))
+        nc.sync.dma_start(n1_sb[:], n1)
+        nc.sync.dma_start(n2_sb[:], n2)
+        nc.sync.dma_start(x_tab[:].bitcast(I32), x_words[0].rearrange("p n t -> p (n t)").bitcast(I32))
+
+        d_scale_picked = keep.tile([P, S], U8, name="d_scale_picked")
+        x_scale_picked = keep.tile([P, S], U8, name="x_scale_picked")
+        planes = keep.tile([P, 2 * S], U8, name="planes", align_bytes=64)
+        nc.vector.tensor_copy(d_scale_picked[:], d_scale_tab[:].indirect(kidx_sb[:]))
+        gn_sb = keep.tile([P, PACK], F32, name="gn_sb", tag="early_small")
+        nc.sync.dma_start(gn_sb[:], gn.rearrange("(p t) o -> p (t o)", t=PACK))
+        nc.vector.tensor_copy(x_scale_picked[:], x_scale_tab[:].indirect(offs_sb[:]))
+        nc.vector.tensor_copy(
+            planes[:, 0:S].rearrange("p (t m) -> p m t", t=PACK),
+            d_scale_picked[:].rearrange("p (m t) -> p m t", t=PACK),
+        )
+        nc.vector.tensor_copy(planes[:, S : 2 * S].bitcast(I32), x_scale_picked[:].bitcast(I32))
+        for c in range(1, 4):
+            nc.scalar.dma_start(planes[c:P:32, :].bitcast(I32), planes[8 * c : P : 32, :].bitcast(I32))
+
+        d_picked = keep.tile([P, S], U32, name="d_picked")
+        d_dealt = keep.tile([P, S], U32, name="d_dealt", align_bytes=64)
+        nc.vector.tensor_copy(d_picked[:], d_tab[:].indirect(kidx_sb[:]))
+        nc.vector.tensor_copy(
+            d_dealt[:].rearrange("p (t c i) -> p c t i", t=PACK, i=LINE),
+            d_picked[:].rearrange("p (c i t) -> p c t i", t=PACK, i=LINE),
+        )
+        w_raw = keep.tile([P, PACK, S], F32, name="w_raw", tag="early_big")
+        nc.sync.dma_start(w_raw[:], w1.rearrange("(p t) m -> p t m", t=PACK))
+        gain = keep.tile([P, PACK], F32, name="gain")
+        nc.scalar.activation(gain[:], gn_sb[:], COPY, scale=0.0625)
+
+        s_banks = [psum.tile([P, S], F32, name="s_bank%d" % t) for t in range(PACK)]
+        s_win = [keep.tile([P, S], F32, name="s_win%d" % t) for t in range(PACK)]
+        s_all = keep.tile([P, PACK, S], F32, name="s_all")
+        for h in range(2):
+            cols = slice(h * HALF, (h + 1) * HALF)
+            x_picked = keep.tile([P, HALF], U32, name="x_picked%d" % h, align_bytes=64)
+            nc.vector.tensor_copy(x_picked[:], x_tab[:].indirect(offs_sb[:, h * 16 : (h + 1) * 16]))
+            for t in range(PACK):
+                nc.tensor.matmul_mx(
+                    s_banks[t][:, cols],
+                    lhsT=d_dealt[:, t * P : (t + 1) * P].bitcast(FP8X4),
+                    lhsT_scale=planes[:, t * P : (t + 1) * P],
+                    rhs=x_picked[:].bitcast(FP8X4),
+                    rhs_scale=planes[:, S + h * HALF : S + (h + 1) * HALF],
+                    start=True,
+                    stop=True,
+                )
+            nc.scalar.activation(s_win[0][:, cols], s_banks[0][:, cols], COPY, scale=gain[:, 0:1])
+
+        s_near = [keep.tile([P, PACK, HALF], F32, name="s_near%d" % h) for h in range(2)]
+        for t in range(PACK):
+            if t > 0:
+                nc.scalar.activation(s_win[t][:], s_banks[t][:], COPY, scale=gain[:, t : t + 1])
+            for h in range(2):
+                nc.vector.tensor_copy(s_near[h][:, t, :], s_win[t][:].indirect(n1_sb[:, h * 16 : (h + 1) * 16]))
+        for t in range(PACK):
+            nc.scalar.activation(s_all[:, t, :], s_banks[t][:], COPY, scale=gain[:, t : t + 1])
+
+        w_bf = keep.tile([P, PACK, P, PACK], BF16, name="w_bf", align_bytes=64)
+        w_codes = keep.tile([P, S], U32, name="w_codes", align_bytes=64)
+        w_plane = keep.tile([P, S], U8, name="w_plane", align_bytes=64)
+        for q in range(4):
+            nc.scalar.copy(
+                w_bf[:, :, 32 * q : 32 * (q + 1), :].rearrange("p u m t -> p m t u"),
+                w_raw[:, :, 128 * q : 128 * (q + 1)].rearrange("p t (m u) -> p m t u", u=PACK),
+            )
+
+        z_codes = []
+        z_planes = []
+        for h in range(2):
+            cols = slice(h * HALF, (h + 1) * HALF)
+            z_bf = keep.tile([P, HALF * PACK], BF16, name="z_bf%d" % h, align_bytes=64)
+            nc.vector.tensor_tensor(
+                z_bf[:].rearrange("p (c i t) -> p c t i", t=PACK, i=LINE),
+                s_all[:, :, cols].rearrange("p t (c i) -> p c t i", i=LINE),
+                s_near[h][:].rearrange("p t (c i) -> p c t i", i=LINE),
+                ALU.subtract,
+            )
+            z_codes.append(keep.tile([P, HALF], U32, name="z_codes%d" % h, align_bytes=64))
+            z_planes.append(keep.tile([P, HALF], U8, name="z_plane%d" % h, align_bytes=64))
+            nc.vector.quantize_mx(z_codes[h][:].bitcast(FP8X4), z_planes[h][:], z_bf[:])
+
+        out_rows = out.rearrange("(p u) j -> p u j", u=PACK)
+        for u in range(PACK):
+            nc.vector.quantize_mx(
+                w_codes[:, u * P : (u + 1) * P].bitcast(FP8X4),
+                w_plane[:, u * P : (u + 1) * P],
+                w_bf[:, u, :, :].rearrange("p m t -> p (m t)"),
+            )
+            h_bank = psum.tile([P, S], F32, name="h_bank%d" % u)
+            h_win = keep.tile([P, S], F32, name="h_win%d" % u)
+            for h in range(2):
+                cols = slice(h * HALF, (h + 1) * HALF)
+                nc.tensor.matmul_mx(
+                    h_bank[:, cols],
+                    lhsT=w_codes[:, u * P : (u + 1) * P].bitcast(FP8X4),
+                    lhsT_scale=w_plane[:, u * P : (u + 1) * P],
+                    rhs=z_codes[h][:].bitcast(FP8X4),
+                    rhs_scale=z_planes[h][:],
+                    start=True,
+                    stop=True,
+                )
+                if u == 0:
+                    nc.scalar.copy(h_win[:, cols], h_bank[:, cols])
+            if u > 0:
+                nc.scalar.copy(h_win[:], h_bank[:])
+            h_near = keep.tile([P, S], F32, name="h_near%d" % u)
+            for h in range(2):
+                cols = slice(h * HALF, (h + 1) * HALF)
+                nc.vector.tensor_copy(h_near[:, cols], h_win[:].indirect(n2_sb[:, h * 16 : (h + 1) * 16]))
+            if u < PACK - 1:
+                res = keep.tile([P, S], F32, name="res%d" % u)
+                nc.vector.tensor_tensor(res[:], h_bank[:], h_near[:], ALU.max)
+                nc.sync.dma_start(out_rows[:, u, :], res[:])
+            else:
+                for h in range(2):
+                    cols = slice(h * HALF, (h + 1) * HALF)
+                    res = keep.tile([P, HALF], F32, name="res%d_%d" % (u, h))
+                    nc.vector.tensor_tensor(res[:], h_bank[:, cols], h_near[:, cols], ALU.max)
+                    nc.sync.dma_start(out_rows[:, u, cols], res[:])

@@ -26,15 +26,26 @@ def tile_picked_keydifbig_none_p_kernel(
     tc, x_words, x_scales, d_words, d_scales, gn, w1, offs, kidx, n1, n2, out
 ):
     nc = tc.nc
+    halves = [slice(0, HALF), slice(HALF, S)]
+    whole = slice(0, S)
     with ExitStack() as ctx:
         lists = ctx.enter_context(tc.tile_pool(name="lists", bufs=1))
         keep = ctx.enter_context(tc.tile_pool(name="keep", bufs=1))
         psum = ctx.enter_context(tc.psum_pool(name="psum", bufs=1))
 
-        d_scale_tab = keep.tile([P, TABLE], U8, name="d_scale_tab", tag="early_small")
+        d_scale_tab = keep.tile([P, TABLE], U8, name="d_scale_tab")
         x_scale_tab = keep.tile([P, TABLE], U8, name="x_scale_tab")
         nc.vector.memset(d_scale_tab[:].bitcast(I32), 0)
-        nc.vector.memset(x_scale_tab[:].bitcast(I32), 0)
+        nc.gpsimd.memset(x_scale_tab[:].bitcast(I32), 0)
+
+        win = [keep.tile([P, 2 * S], F32, name="win%d" % t) for t in range(PACK)]
+        for t in range(PACK):
+            nc.gpsimd.memset(win[t][:, S : 2 * S], 0.0)
+
+        gn_sb = keep.tile([P, PACK], F32, name="gn_sb")
+        nc.scalar.dma_start(gn_sb[:], gn.rearrange("(p t) o -> p (t o)", t=PACK))
+        gain = keep.tile([P, PACK], F32, name="gain")
+        nc.scalar.activation(gain[:], gn_sb[:], COPY, scale=0.0625)
 
         kidx_sb = lists.tile([P, S // 16], U16, name="kidx_sb")
         offs_sb = lists.tile([P, S // 16], U16, name="offs_sb")
@@ -42,23 +53,21 @@ def tile_picked_keydifbig_none_p_kernel(
         n2_sb = lists.tile([P, S // 16], U16, name="n2_sb")
         nc.sync.dma_start(kidx_sb[:], kidx)
         nc.sync.dma_start(offs_sb[:], offs)
-
-        nc.scalar.dma_start(d_scale_tab[0:P:8, :].bitcast(I32), d_scales[0].bitcast(I32))
-        nc.scalar.dma_start(x_scale_tab[0:P:8, :].bitcast(I32), x_scales[0].bitcast(I32))
-
-        d_tab = keep.tile([P, TABLE], U32, name="d_tab", tag="early_big")
-        x_tab = keep.tile([P, TABLE], U32, name="x_tab")
-        nc.sync.dma_start(d_tab[:].bitcast(I32), d_words[0].rearrange("p n t -> p (n t)").bitcast(I32))
         nc.sync.dma_start(n1_sb[:], n1)
         nc.sync.dma_start(n2_sb[:], n2)
+
+        nc.sync.dma_start(d_scale_tab[0:P:8, :].bitcast(I32), d_scales[0].bitcast(I32))
+        nc.sync.dma_start(x_scale_tab[0:P:8, :].bitcast(I32), x_scales[0].bitcast(I32))
+
+        d_tab = keep.tile([P, TABLE], U32, name="d_tab")
+        x_tab = keep.tile([P, TABLE], U32, name="x_tab")
+        nc.sync.dma_start(d_tab[:].bitcast(I32), d_words[0].rearrange("p n t -> p (n t)").bitcast(I32))
         nc.sync.dma_start(x_tab[:].bitcast(I32), x_words[0].rearrange("p n t -> p (n t)").bitcast(I32))
 
         d_scale_picked = keep.tile([P, S], U8, name="d_scale_picked")
-        x_scale_picked = keep.tile([P, S], U8, name="x_scale_picked")
+        x_scale_picked = keep.tile([P, S], U8, name="x_scale_picked", tag="early_big")
         planes = keep.tile([P, 2 * S], U8, name="planes", align_bytes=64)
         nc.vector.tensor_copy(d_scale_picked[:], d_scale_tab[:].indirect(kidx_sb[:]))
-        gn_sb = keep.tile([P, PACK], F32, name="gn_sb", tag="early_small")
-        nc.sync.dma_start(gn_sb[:], gn.rearrange("(p t) o -> p (t o)", t=PACK))
         nc.vector.tensor_copy(x_scale_picked[:], x_scale_tab[:].indirect(offs_sb[:]))
         nc.vector.tensor_copy(
             planes[:, 0:S].rearrange("p (t m) -> p m t", t=PACK),
@@ -67,106 +76,100 @@ def tile_picked_keydifbig_none_p_kernel(
         nc.vector.tensor_copy(planes[:, S : 2 * S].bitcast(I32), x_scale_picked[:].bitcast(I32))
         for c in range(1, 4):
             nc.scalar.dma_start(planes[c:P:32, :].bitcast(I32), planes[8 * c : P : 32, :].bitcast(I32))
+        w_raw = keep.tile([P, PACK, S], F32, name="w_raw", tag="early_big")
+        nc.scalar.dma_start(w_raw[:], w1.rearrange("(p t) m -> p t m", t=PACK))
 
         d_picked = keep.tile([P, S], U32, name="d_picked")
-        d_dealt = keep.tile([P, S], U32, name="d_dealt", align_bytes=64)
+        d_dealt = keep.tile([P, S], U32, name="d_dealt", tag="operand1", align_bytes=64)
         nc.vector.tensor_copy(d_picked[:], d_tab[:].indirect(kidx_sb[:]))
         nc.vector.tensor_copy(
             d_dealt[:].rearrange("p (t c i) -> p c t i", t=PACK, i=LINE),
             d_picked[:].rearrange("p (c i t) -> p c t i", t=PACK, i=LINE),
         )
-        w_raw = keep.tile([P, PACK, S], F32, name="w_raw", tag="early_big")
-        nc.sync.dma_start(w_raw[:], w1.rearrange("(p t) m -> p t m", t=PACK))
-        gain = keep.tile([P, PACK], F32, name="gain")
-        nc.scalar.activation(gain[:], gn_sb[:], COPY, scale=0.0625)
 
-        s_banks = [psum.tile([P, S], F32, name="s_bank%d" % t) for t in range(PACK)]
-        s_win = [keep.tile([P, S], F32, name="s_win%d" % t) for t in range(PACK)]
-        s_all = keep.tile([P, PACK, S], F32, name="s_all")
+        x_picked = keep.tile([P, S], U32, name="x_picked", tag="operand0", align_bytes=64)
         for h in range(2):
-            cols = slice(h * HALF, (h + 1) * HALF)
-            x_picked = keep.tile([P, HALF], U32, name="x_picked%d" % h, align_bytes=64)
-            nc.vector.tensor_copy(x_picked[:], x_tab[:].indirect(offs_sb[:, h * 16 : (h + 1) * 16]))
-            for t in range(PACK):
+            nc.vector.tensor_copy(x_picked[:, halves[h]], x_tab[:].indirect(offs_sb[:, h * 16 : (h + 1) * 16]))
+        s_all = keep.tile([P, PACK, S], F32, name="s_all")
+        s_near = keep.tile([P, PACK, S], F32, name="s_near")
+        for t in range(PACK):
+            for cols in halves if t == 0 else [whole]:
+                s_bank = psum.tile([P, cols.stop - cols.start], F32, name="s_bank%d_%d" % (t, cols.start))
                 nc.tensor.matmul_mx(
-                    s_banks[t][:, cols],
+                    s_bank[:],
                     lhsT=d_dealt[:, t * P : (t + 1) * P].bitcast(FP8X4),
                     lhsT_scale=planes[:, t * P : (t + 1) * P],
-                    rhs=x_picked[:].bitcast(FP8X4),
-                    rhs_scale=planes[:, S + h * HALF : S + (h + 1) * HALF],
+                    rhs=x_picked[:, cols].bitcast(FP8X4),
+                    rhs_scale=planes[:, S + cols.start : S + cols.stop],
                     start=True,
                     stop=True,
                 )
-            nc.scalar.activation(s_win[0][:, cols], s_banks[0][:, cols], COPY, scale=gain[:, 0:1])
+                nc.scalar.activation(win[t][:, cols], s_bank[:], COPY, scale=gain[:, t : t + 1])
+            nc.sync.dma_start(s_all[:, t, :], win[t][:, whole])
+            nc.vector.tensor_copy(s_near[:, t, :], win[t][:].indirect(n1_sb[:]))
 
-        s_near = [keep.tile([P, PACK, HALF], F32, name="s_near%d" % h) for h in range(2)]
-        for t in range(PACK):
-            if t > 0:
-                nc.scalar.activation(s_win[t][:], s_banks[t][:], COPY, scale=gain[:, t : t + 1])
-            for h in range(2):
-                nc.vector.tensor_copy(s_near[h][:, t, :], s_win[t][:].indirect(n1_sb[:, h * 16 : (h + 1) * 16]))
-        for t in range(PACK):
-            nc.scalar.activation(s_all[:, t, :], s_banks[t][:], COPY, scale=gain[:, t : t + 1])
-
-        w_bf = keep.tile([P, PACK, P, PACK], BF16, name="w_bf", align_bytes=64)
+        w_bf = [keep.tile([P, 2, P, PACK], BF16, name="w_bf%d" % v, tag="operand%d" % v, align_bytes=64) for v in range(2)]
         w_codes = keep.tile([P, S], U32, name="w_codes", align_bytes=64)
         w_plane = keep.tile([P, S], U8, name="w_plane", align_bytes=64)
-        for q in range(4):
+        for v in range(2):
             nc.scalar.copy(
-                w_bf[:, :, 32 * q : 32 * (q + 1), :].rearrange("p u m t -> p m t u"),
-                w_raw[:, :, 128 * q : 128 * (q + 1)].rearrange("p t (m u) -> p m t u", u=PACK),
+                w_bf[v][:].rearrange("p u m t -> p m t u"),
+                w_raw[:].rearrange("p t (m u) -> p m t u", u=PACK)[:, :, :, 2 * v : 2 * v + 2],
             )
 
-        z_codes = []
-        z_planes = []
-        for h in range(2):
-            cols = slice(h * HALF, (h + 1) * HALF)
-            z_bf = keep.tile([P, HALF * PACK], BF16, name="z_bf%d" % h, align_bytes=64)
-            nc.vector.tensor_tensor(
-                z_bf[:].rearrange("p (c i t) -> p c t i", t=PACK, i=LINE),
-                s_all[:, :, cols].rearrange("p t (c i) -> p c t i", i=LINE),
-                s_near[h][:].rearrange("p t (c i) -> p c t i", i=LINE),
-                ALU.subtract,
-            )
-            z_codes.append(keep.tile([P, HALF], U32, name="z_codes%d" % h, align_bytes=64))
-            z_planes.append(keep.tile([P, HALF], U8, name="z_plane%d" % h, align_bytes=64))
-            nc.vector.quantize_mx(z_codes[h][:].bitcast(FP8X4), z_planes[h][:], z_bf[:])
-
-        out_rows = out.rearrange("(p u) j -> p u j", u=PACK)
-        for u in range(PACK):
+        def quantize_w(u):
             nc.vector.quantize_mx(
                 w_codes[:, u * P : (u + 1) * P].bitcast(FP8X4),
                 w_plane[:, u * P : (u + 1) * P],
-                w_bf[:, u, :, :].rearrange("p m t -> p (m t)"),
+                w_bf[u // 2][:, u % 2, :, :].rearrange("p m t -> p (m t)"),
             )
-            h_bank = psum.tile([P, S], F32, name="h_bank%d" % u)
-            h_win = keep.tile([P, S], F32, name="h_win%d" % u)
-            for h in range(2):
-                cols = slice(h * HALF, (h + 1) * HALF)
+
+        quantize_w(0)
+        z_bf = [keep.tile([P, HALF * PACK], BF16, name="z_bf%d" % h, align_bytes=64) for h in range(2)]
+        z_codes = keep.tile([P, S], U32, name="z_codes", align_bytes=64)
+        z_plane = keep.tile([P, S], U8, name="z_plane", align_bytes=64)
+        for h in range(2):
+            cols = slice(h * HALF, (h + 1) * HALF)
+            nc.vector.tensor_tensor(
+                z_bf[h][:].rearrange("p (c i t) -> p c t i", t=PACK, i=LINE),
+                s_all[:, :, cols].rearrange("p t (c i) -> p c t i", i=LINE),
+                s_near[:, :, cols].rearrange("p t (c i) -> p c t i", i=LINE),
+                ALU.subtract,
+            )
+        for h in range(2):
+            cols = halves[h]
+            nc.vector.quantize_mx(z_codes[:, cols].bitcast(FP8X4), z_plane[:, cols], z_bf[h][:])
+
+        out_rows = out.rearrange("(p u) j -> p u j", u=PACK)
+        for u in range(PACK):
+            if u > 0:
+                quantize_w(u)
+            h_banks = []
+            for cols in halves if u == 0 else [whole]:
+                tag = "s_bank0_%d" % cols.start if u == 0 else "h_bank%d" % u
+                h_bank = psum.tile([P, cols.stop - cols.start], F32, name="h_bank%d_%d" % (u, cols.start), tag=tag)
+                h_banks.append((cols, h_bank))
                 nc.tensor.matmul_mx(
-                    h_bank[:, cols],
+                    h_bank[:],
                     lhsT=w_codes[:, u * P : (u + 1) * P].bitcast(FP8X4),
                     lhsT_scale=w_plane[:, u * P : (u + 1) * P],
-                    rhs=z_codes[h][:].bitcast(FP8X4),
-                    rhs_scale=z_planes[h][:],
+                    rhs=z_codes[:, cols].bitcast(FP8X4),
+                    rhs_scale=z_plane[:, cols],
                     start=True,
                     stop=True,
                 )
-                if u == 0:
-                    nc.scalar.copy(h_win[:, cols], h_bank[:, cols])
-            if u > 0:
-                nc.scalar.copy(h_win[:], h_bank[:])
+                nc.scalar.copy(win[u][:, cols], h_bank[:])
             h_near = keep.tile([P, S], F32, name="h_near%d" % u)
-            for h in range(2):
-                cols = slice(h * HALF, (h + 1) * HALF)
-                nc.vector.tensor_copy(h_near[:, cols], h_win[:].indirect(n2_sb[:, h * 16 : (h + 1) * 16]))
             if u < PACK - 1:
+                nc.vector.tensor_copy(h_near[:], win[u][:].indirect(n2_sb[:]))
                 res = keep.tile([P, S], F32, name="res%d" % u)
-                nc.vector.tensor_tensor(res[:], h_bank[:], h_near[:], ALU.max)
+                for cols, bank in h_banks:
+                    nc.vector.tensor_tensor(res[:, cols], bank[:], h_near[:, cols], ALU.max)
                 nc.sync.dma_start(out_rows[:, u, :], res[:])
             else:
                 for h in range(2):
-                    cols = slice(h * HALF, (h + 1) * HALF)
+                    cols = halves[h]
+                    nc.vector.tensor_copy(h_near[:, cols], win[u][:].indirect(n2_sb[:, h * 16 : (h + 1) * 16]))
                     res = keep.tile([P, HALF], F32, name="res%d_%d" % (u, h))
                     nc.vector.tensor_tensor(res[:], h_bank[:, cols], h_near[:, cols], ALU.max)
                     nc.sync.dma_start(out_rows[:, u, cols], res[:])

@@ -70,8 +70,8 @@ def tile_picked_keydifbig_none_p_kernel(
         nc.vector.tensor_copy(d_scale_picked[:], d_scale_tab[:].indirect(kidx_sb[:]))
         nc.vector.tensor_copy(x_scale_picked[:], x_scale_tab[:].indirect(offs_sb[:]))
         nc.vector.tensor_copy(
-            planes[:, 0:S].rearrange("p (t m) -> p m t", t=PACK),
-            d_scale_picked[:].rearrange("p (m t) -> p m t", t=PACK),
+            planes[:, 0:S].rearrange("p (t m) -> p t m", t=PACK),
+            d_scale_picked[:].rearrange("p (m t) -> p t m", t=PACK),
         )
         nc.vector.tensor_copy(planes[:, S : 2 * S].bitcast(I32), x_scale_picked[:].bitcast(I32))
         for c in range(1, 4):
@@ -83,8 +83,8 @@ def tile_picked_keydifbig_none_p_kernel(
         d_dealt = keep.tile([P, S], U32, name="d_dealt", tag="operand1", align_bytes=64)
         nc.vector.tensor_copy(d_picked[:], d_tab[:].indirect(kidx_sb[:]))
         nc.vector.tensor_copy(
-            d_dealt[:].rearrange("p (t c i) -> p c t i", t=PACK, i=LINE),
-            d_picked[:].rearrange("p (c i t) -> p c t i", t=PACK, i=LINE),
+            d_dealt[:].rearrange("p (v e c i) -> p c v i e", v=2, e=2, i=LINE),
+            d_picked[:].rearrange("p (c i v e) -> p c v i e", v=2, e=2, i=LINE),
         )
 
         x_picked = keep.tile([P, S], U32, name="x_picked", tag="operand0", align_bytes=64)
@@ -113,8 +113,8 @@ def tile_picked_keydifbig_none_p_kernel(
         w_plane = keep.tile([P, S], U8, name="w_plane", align_bytes=64)
         for v in range(2):
             nc.scalar.copy(
-                w_bf[v][:].rearrange("p u m t -> p m t u"),
-                w_raw[:].rearrange("p t (m u) -> p m t u", u=PACK)[:, :, :, 2 * v : 2 * v + 2],
+                w_bf[v][:].rearrange("p u m t -> p m u t"),
+                w_raw[:].rearrange("p t (m u) -> p m u t", u=PACK)[:, :, 2 * v : 2 * v + 2, :],
             )
 
         def quantize_w(u):
@@ -131,9 +131,9 @@ def tile_picked_keydifbig_none_p_kernel(
         for h in range(2):
             cols = slice(h * HALF, (h + 1) * HALF)
             nc.vector.tensor_tensor(
-                z_bf[h][:].rearrange("p (c i t) -> p c t i", t=PACK, i=LINE),
-                s_all[:, :, cols].rearrange("p t (c i) -> p c t i", i=LINE),
-                s_near[:, :, cols].rearrange("p t (c i) -> p c t i", i=LINE),
+                z_bf[h][:].rearrange("p (c i t) -> p c t i", t=PACK, i=2),
+                s_all[:, :, cols].rearrange("p t (c i) -> p c t i", i=2),
+                s_near[:, :, cols].rearrange("p t (c i) -> p c t i", i=2),
                 ALU.subtract,
             )
         for h in range(2):

@@ -36,11 +36,9 @@ def tile_picked_keydifbig_none_p_kernel(
         d_scale_tab = keep.tile([P, TABLE], U8, name="d_scale_tab")
         x_scale_tab = keep.tile([P, TABLE], U8, name="x_scale_tab")
         nc.vector.memset(d_scale_tab[:].bitcast(I32), 0)
-        nc.gpsimd.memset(x_scale_tab[:].bitcast(I32), 0)
+        nc.vector.memset(x_scale_tab[:].bitcast(I32), 0)
 
-        win = [keep.tile([P, 2 * S], F32, name="win%d" % t) for t in range(PACK)]
-        for t in range(PACK):
-            nc.gpsimd.memset(win[t][:, S : 2 * S], 0.0)
+        win = [keep.tile([P, S], F32, name="win%d" % t) for t in range(PACK)]
 
         gn_sb = keep.tile([P, PACK], F32, name="gn_sb")
         nc.scalar.dma_start(gn_sb[:], gn.rearrange("(p t) o -> p (t o)", t=PACK))
@@ -106,7 +104,8 @@ def tile_picked_keydifbig_none_p_kernel(
                 )
                 nc.scalar.activation(win[t][:, cols], s_bank[:], COPY, scale=gain[:, t : t + 1])
             nc.sync.dma_start(s_all[:, t, :], win[t][:, whole])
-            nc.vector.tensor_copy(s_near[:, t, :], win[t][:].indirect(n1_sb[:]))
+            for h in range(2):
+                nc.vector.tensor_copy(s_near[:, t, halves[h]], win[t][:].indirect(n1_sb[:, h * 16 : (h + 1) * 16]))
 
         w_bf = [keep.tile([P, 2, P, PACK], BF16, name="w_bf%d" % v, tag="operand%d" % v, align_bytes=64) for v in range(2)]
         w_codes = keep.tile([P, S], U32, name="w_codes", align_bytes=64)
@@ -161,7 +160,8 @@ def tile_picked_keydifbig_none_p_kernel(
                 nc.scalar.copy(win[u][:, cols], h_bank[:])
             h_near = keep.tile([P, S], F32, name="h_near%d" % u)
             if u < PACK - 1:
-                nc.vector.tensor_copy(h_near[:], win[u][:].indirect(n2_sb[:]))
+                for h in range(2):
+                    nc.vector.tensor_copy(h_near[:, halves[h]], win[u][:].indirect(n2_sb[:, h * 16 : (h + 1) * 16]))
                 res = keep.tile([P, S], F32, name="res%d" % u)
                 for cols, bank in h_banks:
                     nc.vector.tensor_tensor(res[:, cols], bank[:], h_near[:, cols], ALU.max)

@@ -17,7 +17,11 @@ PACK = 4
 TABLE = 2048
 S = 512
 HALF = S // 2
+GROUP = 16
+BLOCK_ROWS = 8
+QUADRANT = 32
 LINE = 4
+PAIR = 2
 
 FLOPS = 2 * 2 * 512 * 512 * 512
 
@@ -26,8 +30,13 @@ def tile_picked_keydifbig_none_p_kernel(
     tc, x_words, x_scales, d_words, d_scales, gn, w1, offs, kidx, n1, n2, out
 ):
     nc = tc.nc
-    halves = [slice(0, HALF), slice(HALF, S)]
     whole = slice(0, S)
+    halves = [slice(0, HALF), slice(HALF, S)]
+    taper = [slice(0, HALF), slice(HALF, HALF + P), slice(HALF + P, S)]
+
+    def entries(list_tile, cols):
+        return list_tile[:, cols.start // GROUP : cols.stop // GROUP]
+
     with ExitStack() as ctx:
         lists = ctx.enter_context(tc.tile_pool(name="lists", bufs=1))
         keep = ctx.enter_context(tc.tile_pool(name="keep", bufs=1))
@@ -43,19 +52,19 @@ def tile_picked_keydifbig_none_p_kernel(
         gn_sb = keep.tile([P, PACK], F32, name="gn_sb")
         nc.scalar.dma_start(gn_sb[:], gn.rearrange("(p t) o -> p (t o)", t=PACK))
         gain = keep.tile([P, PACK], F32, name="gain")
-        nc.scalar.activation(gain[:], gn_sb[:], COPY, scale=0.0625)
+        nc.scalar.activation(gain[:], gn_sb[:], COPY, scale=-0.0625)
 
-        kidx_sb = lists.tile([P, S // 16], U16, name="kidx_sb")
-        offs_sb = lists.tile([P, S // 16], U16, name="offs_sb")
-        n1_sb = lists.tile([P, S // 16], U16, name="n1_sb")
-        n2_sb = lists.tile([P, S // 16], U16, name="n2_sb")
+        kidx_sb = lists.tile([P, S // GROUP], U16, name="kidx_sb")
+        offs_sb = lists.tile([P, S // GROUP], U16, name="offs_sb")
+        n1_sb = lists.tile([P, S // GROUP], U16, name="n1_sb")
+        n2_sb = lists.tile([P, S // GROUP], U16, name="n2_sb")
         nc.sync.dma_start(kidx_sb[:], kidx)
         nc.sync.dma_start(offs_sb[:], offs)
         nc.sync.dma_start(n1_sb[:], n1)
         nc.sync.dma_start(n2_sb[:], n2)
 
-        nc.sync.dma_start(d_scale_tab[0:P:8, :].bitcast(I32), d_scales[0].bitcast(I32))
-        nc.sync.dma_start(x_scale_tab[0:P:8, :].bitcast(I32), x_scales[0].bitcast(I32))
+        nc.sync.dma_start(d_scale_tab[0:P:BLOCK_ROWS, :].bitcast(I32), d_scales[0].bitcast(I32))
+        nc.sync.dma_start(x_scale_tab[0:P:BLOCK_ROWS, :].bitcast(I32), x_scales[0].bitcast(I32))
 
         d_tab = keep.tile([P, TABLE], U32, name="d_tab")
         x_tab = keep.tile([P, TABLE], U32, name="x_tab")
@@ -63,7 +72,7 @@ def tile_picked_keydifbig_none_p_kernel(
         nc.sync.dma_start(x_tab[:].bitcast(I32), x_words[0].rearrange("p n t -> p (n t)").bitcast(I32))
 
         d_scale_picked = keep.tile([P, S], U8, name="d_scale_picked")
-        x_scale_picked = keep.tile([P, S], U8, name="x_scale_picked", tag="early_big")
+        x_scale_picked = keep.tile([P, S], U8, name="x_scale_picked", tag="before_w_raw")
         planes = keep.tile([P, 2 * S], U8, name="planes", align_bytes=64)
         nc.vector.tensor_copy(d_scale_picked[:], d_scale_tab[:].indirect(kidx_sb[:]))
         nc.vector.tensor_copy(x_scale_picked[:], x_scale_tab[:].indirect(offs_sb[:]))
@@ -72,25 +81,27 @@ def tile_picked_keydifbig_none_p_kernel(
             d_scale_picked[:].rearrange("p (m t) -> p t m", t=PACK),
         )
         nc.vector.tensor_copy(planes[:, S : 2 * S].bitcast(I32), x_scale_picked[:].bitcast(I32))
-        for c in range(1, 4):
-            nc.scalar.dma_start(planes[c:P:32, :].bitcast(I32), planes[8 * c : P : 32, :].bitcast(I32))
-        w_raw = keep.tile([P, PACK, S], F32, name="w_raw", tag="early_big")
+        for c in range(1, QUADRANT // BLOCK_ROWS):
+            nc.scalar.dma_start(
+                planes[c:P:QUADRANT, :].bitcast(I32), planes[BLOCK_ROWS * c : P : QUADRANT, :].bitcast(I32)
+            )
+        w_raw = keep.tile([P, PACK, S], F32, name="w_raw", tag="before_w_raw")
         nc.scalar.dma_start(w_raw[:], w1.rearrange("(p t) m -> p t m", t=PACK))
 
         d_picked = keep.tile([P, S], U32, name="d_picked")
         d_dealt = keep.tile([P, S], U32, name="d_dealt", tag="operand1", align_bytes=64)
         nc.vector.tensor_copy(d_picked[:], d_tab[:].indirect(kidx_sb[:]))
         nc.vector.tensor_copy(
-            d_dealt[:].rearrange("p (v e c i) -> p c v i e", v=2, e=2, i=LINE),
-            d_picked[:].rearrange("p (c i v e) -> p c v i e", v=2, e=2, i=LINE),
+            d_dealt[:].rearrange("p (v e c i) -> p c v i e", v=PAIR, e=PAIR, i=LINE),
+            d_picked[:].rearrange("p (c i v e) -> p c v i e", v=PAIR, e=PAIR, i=LINE),
         )
-
         x_picked = keep.tile([P, S], U32, name="x_picked", tag="operand0", align_bytes=64)
-        for h in range(2):
-            nc.vector.tensor_copy(x_picked[:, halves[h]], x_tab[:].indirect(offs_sb[:, h * 16 : (h + 1) * 16]))
-        s_all = keep.tile([P, PACK, S], F32, name="s_all")
-        s_near = keep.tile([P, PACK, S], F32, name="s_near")
+        for cols in halves:
+            nc.vector.tensor_copy(x_picked[:, cols], x_tab[:].indirect(entries(offs_sb, cols)))
+
+        z_rows = keep.tile([P, PACK, S], F32, name="z_rows")
         for t in range(PACK):
+            s_own = keep.tile([P, S], F32, name="s_own%d" % t)
             for cols in halves if t == 0 else [whole]:
                 s_bank = psum.tile([P, cols.stop - cols.start], F32, name="s_bank%d_%d" % (t, cols.start))
                 nc.tensor.matmul_mx(
@@ -103,51 +114,62 @@ def tile_picked_keydifbig_none_p_kernel(
                     stop=True,
                 )
                 nc.scalar.activation(win[t][:, cols], s_bank[:], COPY, scale=gain[:, t : t + 1])
-            nc.sync.dma_start(s_all[:, t, :], win[t][:, whole])
-            for h in range(2):
-                nc.vector.tensor_copy(s_near[:, t, halves[h]], win[t][:].indirect(n1_sb[:, h * 16 : (h + 1) * 16]))
+                nc.scalar.activation(s_own[:, cols], s_bank[:], COPY, scale=gain[:, t : t + 1])
+            for cols in halves:
+                nc.vector.tensor_tensor(
+                    z_rows[:, t, cols], win[t][:].indirect(entries(n1_sb, cols)), s_own[:, cols], ALU.subtract
+                )
 
-        w_bf = [keep.tile([P, 2, P, PACK], BF16, name="w_bf%d" % v, tag="operand%d" % v, align_bytes=64) for v in range(2)]
+        w_bf = [
+            keep.tile([P, PAIR, P, PACK], BF16, name="w_bf%d" % v, tag="operand%d" % v, align_bytes=64)
+            for v in range(PAIR)
+        ]
         w_codes = keep.tile([P, S], U32, name="w_codes", align_bytes=64)
         w_plane = keep.tile([P, S], U8, name="w_plane", align_bytes=64)
-        for v in range(2):
+        for v in range(PAIR):
             nc.scalar.copy(
-                w_bf[v][:].rearrange("p u m t -> p m u t"),
-                w_raw[:].rearrange("p t (m u) -> p m u t", u=PACK)[:, :, 2 * v : 2 * v + 2, :],
+                w_bf[v][:].rearrange("p e m t -> p m e t"),
+                w_raw[:].rearrange("p t (m u) -> p m u t", u=PACK)[:, :, PAIR * v : PAIR * (v + 1), :],
             )
 
         def quantize_w(u):
             nc.vector.quantize_mx(
                 w_codes[:, u * P : (u + 1) * P].bitcast(FP8X4),
                 w_plane[:, u * P : (u + 1) * P],
-                w_bf[u // 2][:, u % 2, :, :].rearrange("p m t -> p (m t)"),
+                w_bf[u // PAIR][:, u % PAIR, :, :].rearrange("p m t -> p (m t)"),
             )
 
         quantize_w(0)
-        z_bf = [keep.tile([P, HALF * PACK], BF16, name="z_bf%d" % h, align_bytes=64) for h in range(2)]
+
+        z_bf = keep.tile([P, S * PACK], BF16, name="z_bf", align_bytes=64)
         z_codes = keep.tile([P, S], U32, name="z_codes", align_bytes=64)
         z_plane = keep.tile([P, S], U8, name="z_plane", align_bytes=64)
-        for h in range(2):
-            cols = slice(h * HALF, (h + 1) * HALF)
-            nc.vector.tensor_tensor(
-                z_bf[h][:].rearrange("p (c i t) -> p c t i", t=PACK, i=2),
-                s_all[:, :, cols].rearrange("p t (c i) -> p c t i", i=2),
-                s_near[:, :, cols].rearrange("p t (c i) -> p c t i", i=2),
-                ALU.subtract,
-            )
-        for h in range(2):
-            cols = halves[h]
-            nc.vector.quantize_mx(z_codes[:, cols].bitcast(FP8X4), z_plane[:, cols], z_bf[h][:])
 
+        def round_z(cols):
+            nc.vector.tensor_copy(
+                z_bf[:, PACK * cols.start : PACK * cols.stop].rearrange("p (c i t) -> p c t i", t=PACK, i=PAIR),
+                z_rows[:, :, cols].rearrange("p t (c i) -> p c t i", i=PAIR),
+            )
+
+        def quantize_z(cols):
+            nc.vector.quantize_mx(
+                z_codes[:, cols].bitcast(FP8X4), z_plane[:, cols], z_bf[:, PACK * cols.start : PACK * cols.stop]
+            )
+
+        round_z(taper[0])
+        for k in range(1, len(taper)):
+            round_z(taper[k])
+            quantize_z(taper[k - 1])
+        quantize_z(taper[-1])
+
+        freed_banks = ["s_bank0_0", "s_bank0_%d" % HALF, "s_bank1_0"]
         out_rows = out.rearrange("(p u) j -> p u j", u=PACK)
         for u in range(PACK):
             if u > 0:
                 quantize_w(u)
-            h_banks = []
-            for cols in halves if u == 0 else [whole]:
-                tag = "s_bank0_%d" % cols.start if u == 0 else "h_bank%d" % u
-                h_bank = psum.tile([P, cols.stop - cols.start], F32, name="h_bank%d_%d" % (u, cols.start), tag=tag)
-                h_banks.append((cols, h_bank))
+            for k, cols in enumerate(taper if u == 0 else [whole]):
+                tag = freed_banks[k] if u == 0 else "h_bank%d" % u
+                h_bank = psum.tile([P, cols.stop - cols.start], F32, name="h_bank%d_%d" % (u, k), tag=tag)
                 nc.tensor.matmul_mx(
                     h_bank[:],
                     lhsT=w_codes[:, u * P : (u + 1) * P].bitcast(FP8X4),
@@ -160,16 +182,15 @@ def tile_picked_keydifbig_none_p_kernel(
                 nc.scalar.copy(win[u][:, cols], h_bank[:])
             h_near = keep.tile([P, S], F32, name="h_near%d" % u)
             if u < PACK - 1:
-                for h in range(2):
-                    nc.vector.tensor_copy(h_near[:, halves[h]], win[u][:].indirect(n2_sb[:, h * 16 : (h + 1) * 16]))
+                for cols in halves:
+                    nc.vector.tensor_copy(h_near[:, cols], win[u][:].indirect(entries(n2_sb, cols)))
                 res = keep.tile([P, S], F32, name="res%d" % u)
-                for cols, bank in h_banks:
-                    nc.vector.tensor_tensor(res[:, cols], bank[:], h_near[:, cols], ALU.max)
+                nc.vector.tensor_tensor(res[:], win[u][:], h_near[:], ALU.max)
                 nc.sync.dma_start(out_rows[:, u, :], res[:])
             else:
-                for h in range(2):
-                    cols = halves[h]
-                    nc.vector.tensor_copy(h_near[:, cols], win[u][:].indirect(n2_sb[:, h * 16 : (h + 1) * 16]))
-                    res = keep.tile([P, HALF], F32, name="res%d_%d" % (u, h))
-                    nc.vector.tensor_tensor(res[:], h_bank[:, cols], h_near[:, cols], ALU.max)
-                    nc.sync.dma_start(out_rows[:, u, cols], res[:])
+                for k, cols in enumerate(taper):
+                    nc.vector.tensor_copy(h_near[:, cols], win[u][:].indirect(entries(n2_sb, cols)))
+                    res = keep.tile([P, cols.stop - cols.start], F32, name="res%d_%d" % (u, k))
+                    nc.vector.tensor_tensor(res[:], win[u][:, cols], h_near[:, cols], ALU.max)
+                    queue = nc.scalar if k % 2 else nc.sync
+                    queue.dma_start(out_rows[:, u, cols], res[:])

from contextlib import ExitStack

import concourse.mybir as mybir

F32 = mybir.dt.float32
BF16 = mybir.dt.bfloat16
I32 = mybir.dt.int32
U32 = mybir.dt.uint32
U16 = mybir.dt.uint16
U8 = mybir.dt.uint8
FP8X4 = mybir.dt.float8_e4m3fn_x4
COPY = mybir.ActivationFunctionType.Copy
ALU = mybir.AluOpType

P = 128
PACK = 4
TABLE = 2048
S = 512
HALF = S // 2
GROUP = 16
BLOCK_ROWS = 8
QUADRANT = 32
LINE = 4
PAIR = 2

FLOPS = 2 * 2 * 512 * 512 * 512


def tile_picked_keydifbig_none_p_kernel(
    tc, x_words, x_scales, d_words, d_scales, gn, w1, offs, kidx, n1, n2, out
):
    nc = tc.nc
    whole = slice(0, S)
    halves = [slice(0, HALF), slice(HALF, S)]
    taper = [slice(0, HALF), slice(HALF, HALF + P), slice(HALF + P, S)]

    def entries(list_tile, cols):
        return list_tile[:, cols.start // GROUP : cols.stop // GROUP]

    with ExitStack() as ctx:
        lists = ctx.enter_context(tc.tile_pool(name="lists", bufs=1))
        keep = ctx.enter_context(tc.tile_pool(name="keep", bufs=1))
        psum = ctx.enter_context(tc.psum_pool(name="psum", bufs=1))

        d_scale_tab = keep.tile([P, TABLE], U8, name="d_scale_tab")
        x_scale_tab = keep.tile([P, TABLE], U8, name="x_scale_tab")
        nc.vector.memset(d_scale_tab[:].bitcast(I32), 0)
        nc.vector.memset(x_scale_tab[:].bitcast(I32), 0)

        win = [keep.tile([P, S], F32, name="win%d" % t) for t in range(PACK)]

        gn_sb = keep.tile([P, PACK], F32, name="gn_sb")
        nc.scalar.dma_start(gn_sb[:], gn.rearrange("(p t) o -> p (t o)", t=PACK))
        gain = keep.tile([P, PACK], F32, name="gain")
        nc.scalar.activation(gain[:], gn_sb[:], COPY, scale=-0.0625)

        kidx_sb = lists.tile([P, S // GROUP], U16, name="kidx_sb")
        offs_sb = lists.tile([P, S // GROUP], U16, name="offs_sb")
        n1_sb = lists.tile([P, S // GROUP], U16, name="n1_sb")
        n2_sb = lists.tile([P, S // GROUP], U16, name="n2_sb")
        nc.sync.dma_start(kidx_sb[:], kidx)
        nc.sync.dma_start(offs_sb[:], offs)
        nc.sync.dma_start(n1_sb[:], n1)
        nc.sync.dma_start(n2_sb[:], n2)

        nc.sync.dma_start(d_scale_tab[0:P:BLOCK_ROWS, :].bitcast(I32), d_scales[0].bitcast(I32))
        nc.sync.dma_start(x_scale_tab[0:P:BLOCK_ROWS, :].bitcast(I32), x_scales[0].bitcast(I32))

        d_tab = keep.tile([P, TABLE], U32, name="d_tab")
        x_tab = keep.tile([P, TABLE], U32, name="x_tab")
        nc.sync.dma_start(d_tab[:].bitcast(I32), d_words[0].rearrange("p n t -> p (n t)").bitcast(I32))
        nc.sync.dma_start(x_tab[:].bitcast(I32), x_words[0].rearrange("p n t -> p (n t)").bitcast(I32))

        d_scale_picked = keep.tile([P, S], U8, name="d_scale_picked")
        x_scale_picked = keep.tile([P, S], U8, name="x_scale_picked", tag="before_w_raw")
        planes = keep.tile([P, 2 * S], U8, name="planes", align_bytes=64)
        nc.vector.tensor_copy(d_scale_picked[:], d_scale_tab[:].indirect(kidx_sb[:]))
        nc.vector.tensor_copy(x_scale_picked[:], x_scale_tab[:].indirect(offs_sb[:]))
        nc.vector.tensor_copy(
            planes[:, 0:S].rearrange("p (t m) -> p t m", t=PACK),
            d_scale_picked[:].rearrange("p (m t) -> p t m", t=PACK),
        )
        nc.vector.tensor_copy(planes[:, S : 2 * S].bitcast(I32), x_scale_picked[:].bitcast(I32))
        for c in range(1, QUADRANT // BLOCK_ROWS):
            nc.scalar.dma_start(
                planes[c:P:QUADRANT, :].bitcast(I32), planes[BLOCK_ROWS * c : P : QUADRANT, :].bitcast(I32)
            )
        w_raw = keep.tile([P, PACK, S], F32, name="w_raw", tag="before_w_raw")
        nc.scalar.dma_start(w_raw[:], w1.rearrange("(p t) m -> p t m", t=PACK))

        d_picked = keep.tile([P, S], U32, name="d_picked")
        d_dealt = keep.tile([P, S], U32, name="d_dealt", tag="operand1", align_bytes=64)
        nc.vector.tensor_copy(d_picked[:], d_tab[:].indirect(kidx_sb[:]))
        nc.vector.tensor_copy(
            d_dealt[:].rearrange("p (v e c i) -> p c v i e", v=PAIR, e=PAIR, i=LINE),
            d_picked[:].rearrange("p (c i v e) -> p c v i e", v=PAIR, e=PAIR, i=LINE),
        )
        x_picked = keep.tile([P, S], U32, name="x_picked", tag="operand0", align_bytes=64)
        for cols in halves:
            nc.vector.tensor_copy(x_picked[:, cols], x_tab[:].indirect(entries(offs_sb, cols)))

        z_rows = keep.tile([P, PACK, S], F32, name="z_rows")
        for t in range(PACK):
            s_own = keep.tile([P, S], F32, name="s_own%d" % t)
            for cols in halves if t == 0 else [whole]:
                s_bank = psum.tile([P, cols.stop - cols.start], F32, name="s_bank%d_%d" % (t, cols.start))
                nc.tensor.matmul_mx(
                    s_bank[:],
                    lhsT=d_dealt[:, t * P : (t + 1) * P].bitcast(FP8X4),
                    lhsT_scale=planes[:, t * P : (t + 1) * P],
                    rhs=x_picked[:, cols].bitcast(FP8X4),
                    rhs_scale=planes[:, S + cols.start : S + cols.stop],
                    start=True,
                    stop=True,
                )
                nc.scalar.activation(win[t][:, cols], s_bank[:], COPY, scale=gain[:, t : t + 1])
                nc.scalar.activation(s_own[:, cols], s_bank[:], COPY, scale=gain[:, t : t + 1])
            for cols in halves:
                nc.vector.tensor_tensor(
                    z_rows[:, t, cols], win[t][:].indirect(entries(n1_sb, cols)), s_own[:, cols], ALU.subtract
                )

        w_bf = [
            keep.tile([P, PAIR, P, PACK], BF16, name="w_bf%d" % v, tag="operand%d" % v, align_bytes=64)
            for v in range(PAIR)
        ]
        w_codes = keep.tile([P, S], U32, name="w_codes", align_bytes=64)
        w_plane = keep.tile([P, S], U8, name="w_plane", align_bytes=64)
        for v in range(PAIR):
            nc.scalar.copy(
                w_bf[v][:].rearrange("p e m t -> p m e t"),
                w_raw[:].rearrange("p t (m u) -> p m u t", u=PACK)[:, :, PAIR * v : PAIR * (v + 1), :],
            )

        def quantize_w(u):
            nc.vector.quantize_mx(
                w_codes[:, u * P : (u + 1) * P].bitcast(FP8X4),
                w_plane[:, u * P : (u + 1) * P],
                w_bf[u // PAIR][:, u % PAIR, :, :].rearrange("p m t -> p (m t)"),
            )

        quantize_w(0)

        z_bf = keep.tile([P, S * PACK], BF16, name="z_bf", align_bytes=64)
        z_codes = keep.tile([P, S], U32, name="z_codes", align_bytes=64)
        z_plane = keep.tile([P, S], U8, name="z_plane", align_bytes=64)

        def round_z(cols):
            nc.vector.tensor_copy(
                z_bf[:, PACK * cols.start : PACK * cols.stop].rearrange("p (c i t) -> p c t i", t=PACK, i=PAIR),
                z_rows[:, :, cols].rearrange("p t (c i) -> p c t i", i=PAIR),
            )

        def quantize_z(cols):
            nc.vector.quantize_mx(
                z_codes[:, cols].bitcast(FP8X4), z_plane[:, cols], z_bf[:, PACK * cols.start : PACK * cols.stop]
            )

        round_z(taper[0])
        for k in range(1, len(taper)):
            round_z(taper[k])
            quantize_z(taper[k - 1])
        quantize_z(taper[-1])

        freed_banks = ["s_bank0_0", "s_bank0_%d" % HALF, "s_bank1_0"]
        out_rows = out.rearrange("(p u) j -> p u j", u=PACK)
        for u in range(PACK):
            if u > 0:
                quantize_w(u)
            for k, cols in enumerate(taper if u == 0 else [whole]):
                tag = freed_banks[k] if u == 0 else "h_bank%d" % u
                h_bank = psum.tile([P, cols.stop - cols.start], F32, name="h_bank%d_%d" % (u, k), tag=tag)
                nc.tensor.matmul_mx(
                    h_bank[:],
                    lhsT=w_codes[:, u * P : (u + 1) * P].bitcast(FP8X4),
                    lhsT_scale=w_plane[:, u * P : (u + 1) * P],
                    rhs=z_codes[:, cols].bitcast(FP8X4),
                    rhs_scale=z_plane[:, cols],
                    start=True,
                    stop=True,
                )
                nc.scalar.copy(win[u][:, cols], h_bank[:])
            h_near = keep.tile([P, S], F32, name="h_near%d" % u)
            if u < PACK - 1:
                for cols in halves:
                    nc.vector.tensor_copy(h_near[:, cols], win[u][:].indirect(entries(n2_sb, cols)))
                res = keep.tile([P, S], F32, name="res%d" % u)
                nc.vector.tensor_tensor(res[:], win[u][:], h_near[:], ALU.max)
                nc.sync.dma_start(out_rows[:, u, :], res[:])
            else:
                for k, cols in enumerate(taper):
                    nc.vector.tensor_copy(h_near[:, cols], win[u][:].indirect(entries(n2_sb, cols)))
                    res = keep.tile([P, cols.stop - cols.start], F32, name="res%d_%d" % (u, k))
                    nc.vector.tensor_tensor(res[:], win[u][:, cols], h_near[:, cols], ALU.max)
                    queue = nc.scalar if k % 2 else nc.sync
                    queue.dma_start(out_rows[:, u, cols], res[:])
